import numpy as np
import ml_dtypes


def mxq(x, axis, fmt="e4m3"):
    dtype, down = {"e4m3": (ml_dtypes.float8_e4m3fn, 7), "e5m2": (ml_dtypes.float8_e5m2, 14)}[fmt]
    v = np.moveaxis(np.asarray(x, np.float32).astype(ml_dtypes.bfloat16).astype(np.float64), axis, -1)
    blocks = v.reshape(v.shape[:-1] + (-1, 32))
    amax = np.abs(blocks).max(-1, keepdims=True)
    byte = np.maximum(np.where(amax > 0, np.frexp(amax)[1] - 1 + 127, 0) - down, 1)
    scale = np.exp2(byte - 127.0)
    codes = (blocks / scale).astype(np.float32).astype(dtype).astype(np.float64)
    return np.moveaxis((codes * scale).reshape(v.shape), -1, axis)


WIDE = False


def mx_kscale(k):
    if not WIDE:
        return np.ones(k)
    levels = np.array([18, -18])
    if k % 512:
        return np.exp2(np.random.permutation(np.resize(levels, k // 32))).repeat(32)
    a = np.empty((k // 512, 16))
    for p in range(k // 512):
        a[p, :8] = np.random.permutation(np.resize(levels, 8))
        for g in range(8):
            far = levels[np.abs(levels - a[p, g]) >= 10]
            a[p, g + 8] = far[np.random.randint(len(far))]
    return np.exp2(a.ravel()).repeat(32)


def f64(x):
    return np.asarray(x).astype(np.float64)


def striped(idx):
    return np.tile(np.asarray(idx).reshape(-1, 16).T, (8, 1)).astype(np.uint16)


def unstriped(offs):
    return offs[:16].T.reshape(-1).astype(np.int64)


E2M1 = np.array([0.0, 0.5, 1.0, 1.5, 2.0, 3.0, 4.0, 6.0, -0.0, -0.5, -1.0, -1.5, -2.0, -3.0, -4.0, -6.0])


def pack_weight(w, fmt):
    k, n = w.shape
    w = f64(np.asarray(w, np.float32).astype(ml_dtypes.bfloat16)).reshape(k // 32, 32, n)
    amax = np.abs(w).max(1)
    if fmt == "e4m3":
        byte = np.frexp(amax)[1] - 1 + 127 - 7
    else:
        mant, ex = np.frexp(amax / 6.0)
        byte = np.where(mant > 0.5, ex, ex - 1) + 127
    byte = np.clip(np.where(amax > 0, byte, 1), 1, 254)
    scaled = (w * np.exp2(127.0 - byte)[:, None, :]).reshape(k, n).astype(np.float32)
    by_word = np.ascontiguousarray(scaled.reshape(k // 512, 128, 4, n).transpose(0, 1, 3, 2))
    if fmt == "e4m3":
        words = by_word.astype(ml_dtypes.float8_e4m3fn).view(np.uint8)
    else:
        c = by_word.astype(ml_dtypes.float4_e2m1fn).view(np.uint8) & 0xF
        words = (c[..., 0::2] | (c[..., 1::2] << 4)).reshape(k // 512, 128, 2 * n)
    return np.ascontiguousarray(words), np.ascontiguousarray(byte.astype(np.uint8).reshape(k // 512, 16, n))


def unpack_weight(words, scales, fmt):
    g, _, n = scales.shape
    words = np.ascontiguousarray(words).reshape(g, 128, n, -1)
    if fmt == "e4m3":
        vals = words.view(ml_dtypes.float8_e4m3fn).astype(np.float64)
    else:
        nib = np.empty((g, 128, n, 4), np.uint8)
        nib[..., 0::2] = words & 0xF
        nib[..., 1::2] = words >> 4
        vals = E2M1[nib]
    vals = vals * np.repeat(np.exp2(scales.astype(np.float64) - 127.0), 8, axis=1)[..., None]
    return vals.transpose(0, 1, 3, 2).reshape(g * 512, n)


def planes(y):
    n, m = y.shape
    v = y.astype(np.float32).astype(ml_dtypes.bfloat16).astype(np.float64).reshape(n // 32, 32, m)
    top = np.abs(v).max(1)
    byte = np.clip(np.where(top > 0, np.frexp(top)[1] - 1 + 127 - 7, 1), 1, 254)
    codes = (v * np.exp2(127.0 - byte)[:, None, :]).reshape(n, m).astype(np.float32).astype(ml_dtypes.float8_e4m3fn).view(np.uint8)
    words = codes.reshape(n // 512, 128, 4, m).transpose(0, 1, 3, 2)
    return np.ascontiguousarray(words), np.ascontiguousarray(byte.astype(np.uint8).reshape(n // 512, 16, m))


V, K, E, D, DV = 1024, 2, 2048, 512, 512


def setup_inputs():
    n = np.random.standard_normal
    v = mx_kscale(DV)[:, None]
    coarse = lambda x: x.astype(np.float32).astype(ml_dtypes.bfloat16).astype(np.float64)
    wp = pack_weight(n((DV, D)) / np.sqrt(DV) / v, "e2m1")
    return {
        "dyT": (coarse(n((DV, V))) * v).astype(np.float32),
        "hE": (np.random.randint(1, 32, (DV, E)) / 32.0).astype(np.float32),
        "ew": np.tile(np.random.randint(8, 33, E) / 16.0, (128, 1)).astype(np.float32),
        "w_words": wp[0],
        "w_scales": wp[1],
        "offs": striped(np.random.randint(0, V, E)),
        "offs2": striped(np.random.permutation(E)),
    }


def reference(dyT, hE, ew, w_words, w_scales, offs, offs2):
    h = f64(hE)
    dz = f64(ew)[:1] * f64(dyT)[:, unstriped(offs)] * h * (1.0 - h)
    dm = unpack_weight(w_words, w_scales, "e2m1").T @ mxq(dz, 0, "e5m2")
    out_0 = dm[:, unstriped(offs2)].reshape(D, V, K).sum(-1)
    return (out_0,) + planes(out_0)

@@ -1,0 +1,206 @@
+from contextlib import ExitStack
+
+import concourse.mybir as mybir
+
+V, K, E, D, DV = 1024, 2, 2048, 512, 512
+FLOPS = 2 * DV * D * E
+
+F32 = mybir.dt.float32
+BF16 = mybir.dt.bfloat16
+I32 = mybir.dt.int32
+U32 = mybir.dt.uint32
+U16 = mybir.dt.uint16
+U8 = mybir.dt.uint8
+E2M1X4 = mybir.dt.float4_e2m1fn_x4
+E5M2X4 = mybir.dt.float8_e5m2_x4
+E4M3X4 = mybir.dt.float8_e4m3fn_x4
+ALU = mybir.AluOpType
+ACT = mybir.ActivationFunctionType
+
+P = 128
+PACK = 4
+CHUNK = 512
+CHUNKS = E // CHUNK
+PER_COL = 16
+NODE_RUNS = (512, 256, 128, 128)
+
+
+def tile_attend_gmp_pl_sig_ew_kernel(
+    tc, dyT, hE, ew, w_words, w_scales, offs, offs2, out_0, out_1, out_2
+):
+    nc = tc.nc
+    with ExitStack() as ctx:
+        lists = ctx.enter_context(tc.tile_pool(name="lists", bufs=1))
+        keep = ctx.enter_context(tc.tile_pool(name="keep", bufs=1))
+        psum = ctx.enter_context(tc.psum_pool(name="psum", bufs=1))
+
+        dst = lists.tile([P, E // PER_COL], U16, name="dst")
+        src = lists.tile([P, E // PER_COL], U16, name="src")
+
+        dy = [keep.tile([P, V], F32, name=f"dy{t}") for t in range(PACK)]
+        ew_c = [keep.tile([P, CHUNK], F32, name=f"ew{c}") for c in range(CHUNKS)]
+        h = [keep.tile([P, PACK, CHUNK], F32, name=f"h{c}") for c in range(CHUNKS)]
+        slope = h
+        picked = [keep.tile([P, PACK, CHUNK], F32, name=f"picked{c}") for c in range(CHUNKS)]
+        dz = [keep.tile([P, CHUNK, PACK], BF16, name=f"dz{c}", align_bytes=64) for c in range(CHUNKS)]
+        dz_codes = [keep.tile([P, CHUNK], U32, name=f"dzc{c}", align_bytes=64) for c in range(CHUNKS)]
+        dz_scales = [keep.tile([P, CHUNK], U8, name=f"dzs{c}", align_bytes=64) for c in range(CHUNKS)]
+        dm = [keep.tile([P, E], F32, name=f"dm{t}") for t in range(PACK)]
+        w_raw = keep.tile([P, 2 * D], U8, name="w_raw")
+        ws_raw = keep.tile([P, D], U8, name="ws_raw")
+        w_dealt = keep.tile([P, 2 * D], U8, name="w_dealt", align_bytes=64)
+        ws_dealt = keep.tile([P, D], U8, name="ws_dealt", align_bytes=64)
+        minus_half = keep.tile([P, 1], F32, name="minus_half")
+        quarter = keep.tile([P, 1], F32, name="quarter")
+
+        dy_rows = dyT.rearrange("(p t) v -> p t v", t=PACK)
+        h_rows = hE.rearrange("(p t) e -> p t e", t=PACK)
+
+        def edges(c):
+            return slice(c * CHUNK, (c + 1) * CHUNK)
+
+        nc.gpsimd.memset(ws_raw[:].bitcast(I32), 0)
+        nc.gpsimd.memset(minus_half[:], -0.5)
+        nc.scalar.activation(quarter[:], minus_half[:], ACT.Square)
+
+        nc.sync.dma_start(dst[:], offs)
+        nc.sync.dma_start(ew_c[0][:], ew[:, edges(0)])
+        nc.sync.dma_start(dy[0][:], dy_rows[:, 0, :])
+        nc.scalar.dma_start(w_raw[:].bitcast(I32), w_words[0].bitcast(I32))
+        for q in range(4):
+            nc.scalar.dma_start(
+                ws_raw[32 * q : 32 * q + 4, :].bitcast(I32), w_scales[0, 4 * q : 4 * q + 4, :].bitcast(I32)
+            )
+        for c in range(1, CHUNKS):
+            nc.sync.dma_start(ew_c[c][:], ew[:, edges(c)])
+        for c in range(CHUNKS):
+            nc.sync.dma_start(h[c][:], h_rows[:, :, edges(c)])
+            if c + 1 < PACK:
+                nc.sync.dma_start(dy[c + 1][:], dy_rows[:, c + 1, :])
+        nc.sync.dma_start(src[:], offs2)
+
+        nc.vector.tensor_copy(
+            w_dealt[:].bitcast(U16).rearrange("p (t m) -> p t m", t=PACK),
+            w_raw[:].bitcast(U16).rearrange("p (m t) -> p t m", t=PACK),
+        )
+        nc.vector.tensor_copy(
+            ws_dealt[:].rearrange("p (t m) -> p t m", t=PACK),
+            ws_raw[:].rearrange("p (m t) -> p t m", t=PACK),
+        )
+
+        for c in range(CHUNKS):
+            nc.scalar.activation(slope[c][:], h[c][:], ACT.Square, bias=minus_half[:])
+            nc.scalar.activation(slope[c][:], slope[c][:], ACT.Identity, bias=quarter[:], scale=-1.0)
+
+        def gather_dy(c, t):
+            cols = slice(c * CHUNK // PER_COL, (c + 1) * CHUNK // PER_COL)
+            nc.vector.tensor_tensor(picked[c][:, t, :], dy[t][:].indirect(dst[:, cols]), ew_c[c][:], ALU.mult)
+
+        def form_dz(c, lo, hi):
+            nc.vector.tensor_tensor(
+                dz[c][:, lo:hi, :].rearrange("p (c i) t -> p c t i", i=2),
+                picked[c][:, :, lo:hi].rearrange("p t (c i) -> p c t i", i=2),
+                slope[c][:, :, lo:hi].rearrange("p t (c i) -> p c t i", i=2),
+                ALU.mult,
+            )
+
+        def quantise_dz(c, lo, hi):
+            nc.vector.quantize_mx(
+                dz_codes[c][:, lo:hi].bitcast(E5M2X4),
+                dz_scales[c][:, lo:hi],
+                dz[c][:, lo:hi, :].rearrange("p e t -> p (e t)"),
+            )
+
+        def multiply(c):
+            for t in range(PACK):
+                acc = psum.tile([P, CHUNK], F32, name=f"acc{(c % 2) * PACK + t}")
+                nc.tensor.matmul_mx(
+                    acc[:],
+                    lhsT=w_dealt[:, t * 2 * P : (t + 1) * 2 * P].bitcast(E2M1X4),
+                    lhsT_scale=ws_dealt[:, t * P : (t + 1) * P],
+                    rhs=dz_codes[c][:].bitcast(E5M2X4),
+                    rhs_scale=dz_scales[c][:],
+                    start=True,
+                    stop=True,
+                )
+                nc.scalar.copy(dm[t][:, edges(c)], acc[:])
+
+        for t in range(PACK - 1):
+            for c in range(CHUNKS):
+                gather_dy(c, t)
+        last = CHUNKS - 1
+        gather_dy(0, PACK - 1)
+        gather_dy(1, PACK - 1)
+        form_dz(0, 0, CHUNK)
+        gather_dy(2, PACK - 1)
+        quantise_dz(0, 0, CHUNK)
+        multiply(0)
+        form_dz(1, 0, CHUNK)
+        gather_dy(3, PACK - 1)
+        quantise_dz(1, 0, CHUNK)
+        multiply(1)
+        form_dz(2, 0, CHUNK)
+        form_dz(last, 0, 256)
+        quantise_dz(2, 0, CHUNK)
+        multiply(2)
+        form_dz(last, 256, 384)
+        quantise_dz(last, 0, 256)
+        form_dz(last, 384, 512)
+        quantise_dz(last, 256, 384)
+        quantise_dz(last, 384, 512)
+        multiply(last)
+
+        y_codes = keep.tile([P, V], U32, name="y_codes", align_bytes=64)
+        y_scales = keep.tile([P, V], U8, name="y_scales", align_bytes=64)
+        y_rows = out_0.rearrange("(p t) x -> p t x", t=PACK)
+        code_rows = out_1[0].rearrange("p x l -> p (x l)").bitcast(I32)
+
+        starts = [sum(NODE_RUNS[:r]) for r in range(len(NODE_RUNS))]
+        pairs = [keep.tile([P, PACK, K * n], F32, name=f"pairs{r}") for r, n in enumerate(NODE_RUNS)]
+        y = [keep.tile([P, PACK, n], F32, name=f"y{r}") for r, n in enumerate(NODE_RUNS)]
+        y_bf = [keep.tile([P, n, PACK], BF16, name=f"ybf{r}", align_bytes=64) for r, n in enumerate(NODE_RUNS)]
+
+        def gather_dm(r, t):
+            cols = slice(K * starts[r] // PER_COL, K * (starts[r] + NODE_RUNS[r]) // PER_COL)
+            nc.vector.tensor_copy(pairs[r][:, t, :], dm[t][:].indirect(src[:, cols]))
+
+        def add_pairs(r):
+            both = pairs[r][:].rearrange("p t (x j) -> p (t x) j", j=K)
+            nc.vector.tensor_tensor(
+                y[r][:].rearrange("p t x -> p (t x)"), both[:, :, 0], both[:, :, 1], ALU.add
+            )
+            nodes = slice(starts[r], starts[r] + NODE_RUNS[r])
+            nc.sync.dma_start(y_rows[:, :, nodes], y[r][:])
+
+        def round_y(r, copy):
+            copy(
+                y_bf[r][:].rearrange("p (c i) t -> p c t i", i=2),
+                y[r][:].rearrange("p t (c i) -> p c t i", i=2),
+            )
+
+        def quantise_y(r):
+            nodes = slice(starts[r], starts[r] + NODE_RUNS[r])
+            nc.vector.quantize_mx(
+                y_codes[:, nodes].bitcast(E4M3X4), y_scales[:, nodes], y_bf[r][:].rearrange("p x t -> p (x t)")
+            )
+            nc.sync.dma_start(code_rows[:, nodes], y_codes[:, nodes].bitcast(I32))
+
+        runs = len(NODE_RUNS)
+        for r in range(runs):
+            gather_dm(r, 0)
+            if r > 0:
+                add_pairs(r - 1)
+                round_y(r - 1, nc.scalar.copy)
+            for t in range(1, PACK):
+                gather_dm(r, t)
+            if r > 1:
+                quantise_y(r - 2)
+        add_pairs(runs - 1)
+        quantise_y(runs - 2)
+        round_y(runs - 1, nc.vector.tensor_copy)
+        quantise_y(runs - 1)
+        for q in range(4):
+            queue = nc.scalar if q % 2 == 0 else nc.sync
+            queue.dma_start(
+                out_2[0, 4 * q : 4 * q + 4, :].bitcast(I32), y_scales[32 * q : 32 * q + 4, :].bitcast(I32)
+            )

@@ -1,6 +1,7 @@
 from contextlib import ExitStack
 
 import concourse.mybir as mybir
+from concourse.masks import make_identity
 
 V, K, E, D, DV = 1024, 2, 2048, 512, 512
 FLOPS = 2 * DV * D * E
@@ -20,9 +21,11 @@ ACT = mybir.ActivationFunctionType
 P = 128
 PACK = 4
 CHUNK = 512
-CHUNKS = E // CHUNK
+HALF = CHUNK // 2
 PER_COL = 16
-NODE_RUNS = (512, 256, 128, 128)
+A0, B0, B1, A1 = 0, 1, 2, 3
+NODE_RUNS = (256, 256, 256, 128, 128)
+TURNED_RUNS = 3
 
 
 def tile_attend_gmp_pl_sig_ew_kernel(
@@ -34,24 +37,30 @@ def tile_attend_gmp_pl_sig_ew_kernel(
         keep = ctx.enter_context(tc.tile_pool(name="keep", bufs=1))
         psum = ctx.enter_context(tc.psum_pool(name="psum", bufs=1))
 
+        def sb(shape, dtype, name):
+            return keep.tile(shape, dtype, name=name, align_bytes=64)
+
+        def bank(shape, number):
+            return psum.tile(shape, F32, name=f"bank{number}")
+
         dst = lists.tile([P, E // PER_COL], U16, name="dst")
         src = lists.tile([P, E // PER_COL], U16, name="src")
 
-        dy = [keep.tile([P, V], F32, name=f"dy{t}") for t in range(PACK)]
-        ew_c = [keep.tile([P, CHUNK], F32, name=f"ew{c}") for c in range(CHUNKS)]
-        h = [keep.tile([P, PACK, CHUNK], F32, name=f"h{c}") for c in range(CHUNKS)]
-        slope = h
-        picked = [keep.tile([P, PACK, CHUNK], F32, name=f"picked{c}") for c in range(CHUNKS)]
-        dz = [keep.tile([P, CHUNK, PACK], BF16, name=f"dz{c}", align_bytes=64) for c in range(CHUNKS)]
-        dz_codes = [keep.tile([P, CHUNK], U32, name=f"dzc{c}", align_bytes=64) for c in range(CHUNKS)]
-        dz_scales = [keep.tile([P, CHUNK], U8, name=f"dzs{c}", align_bytes=64) for c in range(CHUNKS)]
-        dm = [keep.tile([P, E], F32, name=f"dm{t}") for t in range(PACK)]
-        w_raw = keep.tile([P, 2 * D], U8, name="w_raw")
-        ws_raw = keep.tile([P, D], U8, name="ws_raw")
-        w_dealt = keep.tile([P, 2 * D], U8, name="w_dealt", align_bytes=64)
-        ws_dealt = keep.tile([P, D], U8, name="ws_dealt", align_bytes=64)
-        minus_half = keep.tile([P, 1], F32, name="minus_half")
-        quarter = keep.tile([P, 1], F32, name="quarter")
+        dy = [sb([P, V], F32, f"dy{t}") for t in range(PACK)]
+        ew_rows = {c: sb([P, CHUNK], F32, f"ew{c}") for c in (A0, A1)}
+        square = {c: sb([P, PACK, CHUNK], F32, f"square{c}") for c in (A0, A1)}
+        slope = {(c, t): sb([P, CHUNK], F32, f"slope{c}_{t}") for c in (B0, B1) for t in range(PACK)}
+        dz_scales = {c: sb([P, CHUNK], U8, f"dzs{c}") for c in (A0, A1, B0, B1)}
+        dm = [sb([P, E], F32, f"dm{t}") for t in range(PACK)]
+        w_raw = sb([P, 2 * D], U8, "w_raw")
+        ws_raw = sb([P, D], U8, "ws_raw")
+        w_dealt = sb([P, 2 * D], U8, "w_dealt")
+        ws_dealt = sb([P, D], U8, "ws_dealt")
+        ew_blocks = sb([P, P], F32, "ew_blocks")
+        ew_cols = sb([P, E // P], F32, "ew_cols")
+        minus_half = sb([P, 1], F32, "minus_half")
+        quarter = sb([P, 1], F32, "quarter")
+        identity = sb([P, P], F32, "identity")
 
         dy_rows = dyT.rearrange("(p t) v -> p t v", t=PACK)
         h_rows = hE.rearrange("(p t) e -> p t e", t=PACK)
@@ -61,22 +70,38 @@ def tile_attend_gmp_pl_sig_ew_kernel(
 
         nc.gpsimd.memset(ws_raw[:].bitcast(I32), 0)
         nc.gpsimd.memset(minus_half[:], -0.5)
+        make_identity(nc, identity[:])
         nc.scalar.activation(quarter[:], minus_half[:], ACT.Square)
 
+        def load_dy(t):
+            nc.sync.dma_start(dy[t][:], dy_rows[:, t, :])
+
+        def load_h_plane(c, t):
+            nc.sync.dma_start(slope[c, t][:], h_rows[:, t, edges(c)])
+
         nc.sync.dma_start(dst[:], offs)
-        nc.sync.dma_start(ew_c[0][:], ew[:, edges(0)])
-        nc.sync.dma_start(dy[0][:], dy_rows[:, 0, :])
+        nc.sync.dma_start(ew_rows[A0][:], ew[:, edges(A0)])
+        load_dy(0)
         nc.scalar.dma_start(w_raw[:].bitcast(I32), w_words[0].bitcast(I32))
         for q in range(4):
             nc.scalar.dma_start(
                 ws_raw[32 * q : 32 * q + 4, :].bitcast(I32), w_scales[0, 4 * q : 4 * q + 4, :].bitcast(I32)
             )
-        for c in range(1, CHUNKS):
-            nc.sync.dma_start(ew_c[c][:], ew[:, edges(c)])
-        for c in range(CHUNKS):
-            nc.sync.dma_start(h[c][:], h_rows[:, :, edges(c)])
-            if c + 1 < PACK:
-                nc.sync.dma_start(dy[c + 1][:], dy_rows[:, c + 1, :])
+        nc.sync.dma_start(ew_rows[A1][:], ew[:, edges(A1)])
+        load_h_plane(B0, 0)
+        load_h_plane(B0, 1)
+        load_dy(1)
+        load_h_plane(B0, 2)
+        load_h_plane(B0, 3)
+        nc.sync.dma_start(square[A0][:], h_rows[:, :, edges(A0)])
+        load_dy(2)
+        nc.sync.dma_start(ew_blocks[:], ew[0:8, :].rearrange("q (c p) -> (q c) p", p=P))
+        load_h_plane(B1, 0)
+        load_h_plane(B1, 1)
+        load_h_plane(B1, 2)
+        load_h_plane(B1, 3)
+        load_dy(3)
+        nc.sync.dma_start(square[A1][:], h_rows[:, :, edges(A1)])
         nc.sync.dma_start(src[:], offs2)
 
         nc.vector.tensor_copy(
@@ -88,117 +113,237 @@ def tile_attend_gmp_pl_sig_ew_kernel(
             ws_raw[:].rearrange("p (m t) -> p t m", t=PACK),
         )
 
-        for c in range(CHUNKS):
-            nc.scalar.activation(slope[c][:], h[c][:], ACT.Square, bias=minus_half[:])
-            nc.scalar.activation(slope[c][:], slope[c][:], ACT.Identity, bias=quarter[:], scale=-1.0)
-
-        def gather_dy(c, t):
-            cols = slice(c * CHUNK // PER_COL, (c + 1) * CHUNK // PER_COL)
-            nc.vector.tensor_tensor(picked[c][:, t, :], dy[t][:].indirect(dst[:, cols]), ew_c[c][:], ALU.mult)
-
-        def form_dz(c, lo, hi):
-            nc.vector.tensor_tensor(
-                dz[c][:, lo:hi, :].rearrange("p (c i) t -> p c t i", i=2),
-                picked[c][:, :, lo:hi].rearrange("p t (c i) -> p c t i", i=2),
-                slope[c][:, :, lo:hi].rearrange("p t (c i) -> p c t i", i=2),
-                ALU.mult,
-            )
-
-        def quantise_dz(c, lo, hi):
-            nc.vector.quantize_mx(
-                dz_codes[c][:, lo:hi].bitcast(E5M2X4),
-                dz_scales[c][:, lo:hi],
-                dz[c][:, lo:hi, :].rearrange("p e t -> p (e t)"),
-            )
-
-        def multiply(c):
+        def form_square(c):
             for t in range(PACK):
-                acc = psum.tile([P, CHUNK], F32, name=f"acc{(c % 2) * PACK + t}")
-                nc.tensor.matmul_mx(
-                    acc[:],
-                    lhsT=w_dealt[:, t * 2 * P : (t + 1) * 2 * P].bitcast(E2M1X4),
-                    lhsT_scale=ws_dealt[:, t * P : (t + 1) * P],
-                    rhs=dz_codes[c][:].bitcast(E5M2X4),
-                    rhs_scale=dz_scales[c][:],
-                    start=True,
-                    stop=True,
+                nc.scalar.activation(square[c][:, t, :], square[c][:, t, :], ACT.Square, bias=minus_half[:])
+
+        def form_slope(c):
+            for t in range(PACK):
+                nc.scalar.activation(slope[c, t][:], slope[c, t][:], ACT.Square, bias=minus_half[:])
+                nc.scalar.activation(slope[c, t][:], slope[c, t][:], ACT.Identity, bias=quarter[:], scale=-1.0)
+
+        for c in (A0, A1):
+            nc.scalar.activation(ew_rows[c][:], ew_rows[c][:], ACT.Copy, scale=-1.0)
+        form_slope(B0)
+        form_square(A0)
+        ew_turned = bank([P, P], 7)
+        nc.tensor.transpose(ew_turned[:], ew_blocks[:], identity[:])
+        nc.scalar.copy(ew_cols[:], ew_turned[:, 0 : E // P])
+        form_slope(B1)
+
+        def listed(c):
+            return dst[:, c * CHUNK // PER_COL : (c + 1) * CHUNK // PER_COL]
+
+        picked = {c: sb([P, PACK, CHUNK], F32, f"picked{c}") for c in (A0, A1)}
+        dz_codes = {}
+        dz_whole = {}
+        dz_half = {}
+        by_edge = {}
+        rounded = {}
+
+        def gather_times_weight(c, t):
+            nc.vector.tensor_tensor(picked[c][:, t, :], dy[t][:].indirect(listed(c)), ew_rows[c][:], ALU.mult)
+
+        def gather_times_slope(c, t, slot):
+            unweighted = sb([P, CHUNK], F32, slot)
+            nc.vector.tensor_tensor(unweighted[:], dy[t][:].indirect(listed(c)), slope[c, t][:], ALU.mult)
+            for b in range(CHUNK // P):
+                if (c, b) not in by_edge:
+                    by_edge[c, b] = bank([P, PACK, P], b)
+                nc.tensor.transpose(by_edge[c, b][:, t, :], unweighted[:, b * P : (b + 1) * P], identity[:])
+
+        def form_dz_direct(c, slot):
+            word_planes = sb([P, 2, CHUNK, 2], BF16, slot)
+            for u in range(2):
+                nc.vector.scalar_tensor_tensor(
+                    word_planes[:, u, :, :],
+                    square[c][:, 2 * u : 2 * u + 2, :].rearrange("p i e -> p e i"),
+                    -0.25,
+                    picked[c][:, 2 * u : 2 * u + 2, :].rearrange("p i e -> p e i"),
+                    ALU.add,
+                    ALU.mult,
                 )
-                nc.scalar.copy(dm[t][:, edges(c)], acc[:])
+            dz_whole[c] = sb([P, CHUNK, PACK], BF16, f"dz{c}")
+            nc.vector.tensor_copy(
+                dz_whole[c][:].rearrange("p e t -> p (e t)").bitcast(I32).rearrange("p (e u) -> p e u", u=2),
+                word_planes[:].rearrange("p u e i -> p (u e i)").bitcast(I32).rearrange("p (u e) -> p e u", u=2),
+            )
 
-        for t in range(PACK - 1):
-            for c in range(CHUNKS):
-                gather_dy(c, t)
-        last = CHUNKS - 1
-        gather_dy(0, PACK - 1)
-        gather_dy(1, PACK - 1)
-        form_dz(0, 0, CHUNK)
-        gather_dy(2, PACK - 1)
-        quantise_dz(0, 0, CHUNK)
-        multiply(0)
-        form_dz(1, 0, CHUNK)
-        gather_dy(3, PACK - 1)
-        quantise_dz(1, 0, CHUNK)
-        multiply(1)
-        form_dz(2, 0, CHUNK)
-        form_dz(last, 0, 256)
-        quantise_dz(2, 0, CHUNK)
-        multiply(2)
-        form_dz(last, 256, 384)
-        quantise_dz(last, 0, 256)
-        form_dz(last, 384, 512)
-        quantise_dz(last, 256, 384)
-        quantise_dz(last, 384, 512)
-        multiply(last)
+        def form_dz_turned(c):
+            for half in range(2):
+                words = bank([P, 2, 2, P], 4 + half)
+                for bb in range(2):
+                    b = 2 * half + bb
+                    rounded[c, b] = sb([P, 2, P, 2], BF16, f"rounded{c}_{b}")
+                    column = c * (CHUNK // P) + b
+                    nc.scalar.activation(
+                        rounded[c, b][:],
+                        by_edge[c, b][:].rearrange("e (u i) p -> e u p i", i=2),
+                        ACT.Copy,
+                        scale=ew_cols[:, column : column + 1],
+                    )
+                    as_words = rounded[c, b][:].rearrange("e u p i -> e (u p i)").bitcast(F32)
+                    for u in range(2):
+                        nc.tensor.transpose(words[:, bb, u, :], as_words[:, u * P : (u + 1) * P], identity[:])
+                dz_half[c, half] = sb([P, HALF, PACK], BF16, f"dz{c}_{half}")
+                nc.scalar.copy(
+                    dz_half[c, half][:]
+                    .rearrange("p e t -> p (e t)")
+                    .bitcast(F32)
+                    .rearrange("p (b e u) -> p b e u", b=2, u=2),
+                    words[:].rearrange("p b u e -> p b e u"),
+                )
 
-        y_codes = keep.tile([P, V], U32, name="y_codes", align_bytes=64)
-        y_scales = keep.tile([P, V], U8, name="y_scales", align_bytes=64)
+        def quantise_whole(c, slot):
+            dz_codes[c] = sb([P, CHUNK], U32, slot)
+            nc.vector.quantize_mx(
+                dz_codes[c][:].bitcast(E5M2X4), dz_scales[c][:], dz_whole[c][:].rearrange("p e t -> p (e t)")
+            )
+
+        def quantise_half(c, half):
+            if half == 0:
+                dz_codes[c] = sb([P, CHUNK], U32, f"dzc{c}")
+            cols = slice(half * HALF, (half + 1) * HALF)
+            nc.vector.quantize_mx(
+                dz_codes[c][:, cols].bitcast(E5M2X4),
+                dz_scales[c][:, cols],
+                dz_half[c, half][:].rearrange("p e t -> p (e t)"),
+            )
+
+        def multiply(c, t, number, copy):
+            acc = bank([P, CHUNK], number)
+            nc.tensor.matmul_mx(
+                acc[:],
+                lhsT=w_dealt[:, t * 2 * P : (t + 1) * 2 * P].bitcast(E2M1X4),
+                lhsT_scale=ws_dealt[:, t * P : (t + 1) * P],
+                rhs=dz_codes[c][:].bitcast(E5M2X4),
+                rhs_scale=dz_scales[c][:],
+                start=True,
+                stop=True,
+            )
+            copy(dm[t][:, edges(c)], acc[:])
+
+        for t in range(PACK):
+            if t == PACK - 1:
+                gather_times_slope(B0, t, f"unweighted{t}")
+            gather_times_weight(A0, t)
+            gather_times_weight(A1, t)
+            if t < PACK - 1:
+                gather_times_slope(B0, t, f"unweighted{t}")
+        form_dz_turned(B0)
+        form_square(A1)
+        form_dz_direct(A0, f"slope{B0}_3")
+        quantise_half(B0, 0)
+        quantise_whole(A0, f"rounded{B0}_3")
+        quantise_half(B0, 1)
+        for t in range(PACK):
+            multiply(A0, t, 4 + t, nc.scalar.copy)
+        for t in range(PACK):
+            multiply(B0, t, t, nc.scalar.copy)
+        gather_times_slope(B1, 1, f"dz{B0}_0")
+        gather_times_slope(B1, 0, f"dz{A0}")
+        gather_times_slope(B1, 2, f"dz{B0}_1")
+        gather_times_slope(B1, 3, f"slope{B1}_0")
+        form_dz_turned(B1)
+        form_dz_direct(A1, f"slope{B1}_2")
+        quantise_half(B1, 0)
+        quantise_whole(A1, f"rounded{B1}_2")
+        quantise_half(B1, 1)
+        for t in range(PACK):
+            multiply(A1, t, 6 + t % 2, nc.scalar.copy)
+            multiply(B1, t, 2 + t, nc.vector.tensor_copy if t == 0 else nc.scalar.copy)
+
+        y_codes = sb([P, V], U32, "y_codes")
+        y_scales = sb([P, V], U8, "y_scales")
         y_rows = out_0.rearrange("(p t) x -> p t x", t=PACK)
         code_rows = out_1[0].rearrange("p x l -> p (x l)").bitcast(I32)
 
         starts = [sum(NODE_RUNS[:r]) for r in range(len(NODE_RUNS))]
-        pairs = [keep.tile([P, PACK, K * n], F32, name=f"pairs{r}") for r, n in enumerate(NODE_RUNS)]
-        y = [keep.tile([P, PACK, n], F32, name=f"y{r}") for r, n in enumerate(NODE_RUNS)]
-        y_bf = [keep.tile([P, n, PACK], BF16, name=f"ybf{r}", align_bytes=64) for r, n in enumerate(NODE_RUNS)]
+        y = [sb([P, PACK, n], F32, f"y{r}") for r, n in enumerate(NODE_RUNS)]
+        pairs = {}
+        y_bf = {}
+        sums = {}
 
-        def gather_dm(r, t):
+        def nodes(r):
+            return slice(starts[r], starts[r] + NODE_RUNS[r])
+
+        def gather_dm(r, t, slot):
+            pairs[r, t] = sb([P, K * NODE_RUNS[r]], F32, slot)
             cols = slice(K * starts[r] // PER_COL, K * (starts[r] + NODE_RUNS[r]) // PER_COL)
-            nc.vector.tensor_copy(pairs[r][:, t, :], dm[t][:].indirect(src[:, cols]))
+            nc.vector.tensor_copy(pairs[r, t][:], dm[t][:].indirect(src[:, cols]))
 
-        def add_pairs(r):
-            both = pairs[r][:].rearrange("p t (x j) -> p (t x) j", j=K)
-            nc.vector.tensor_tensor(
-                y[r][:].rearrange("p t x -> p (t x)"), both[:, :, 0], both[:, :, 1], ALU.add
-            )
-            nodes = slice(starts[r], starts[r] + NODE_RUNS[r])
-            nc.sync.dma_start(y_rows[:, :, nodes], y[r][:])
+        def add_turned(r, t):
+            if t % 2 == 0:
+                sums[r, t // 2] = bank([P, 2, 2, P], (7, 5)[t // 2])
+            for b in range(2):
+                for j in range(K):
+                    nc.tensor.matmul(
+                        sums[r, t // 2][:, t % 2, b, :],
+                        lhsT=pairs[r, t][:, b * K * P + j : (b + 1) * K * P : K],
+                        rhs=identity[:],
+                        is_transpose=True,
+                        start=(j == 0),
+                        stop=(j == K - 1),
+                    )
+
+        def turn_back(r, u):
+            by_node = sb([P, 2 * 2, P], F32, f"by_node{u}")
+            nc.scalar.copy(by_node[:], sums[r, u][:].rearrange("x i b p -> x (i b) p"))
+            back = bank([P, 2 * 2, P], u)
+            for piece in range(2 * 2):
+                nc.tensor.transpose(back[:, piece, :], by_node[:, piece, :], identity[:])
+            nc.scalar.copy(y[r][:, 2 * u : 2 * u + 2, :], back[:].rearrange("p (i b) x -> p i (b x)", i=2))
+
+        def add_pairs(r, t):
+            both = pairs[r, t][:].rearrange("p (x j) -> p x j", j=K)
+            nc.vector.tensor_tensor(y[r][:, t, :], both[:, :, 0], both[:, :, 1], ALU.add)
 
         def round_y(r, copy):
+            if r == final:
+                y_bf[r] = sb([P, NODE_RUNS[r], PACK], BF16, f"ybf{r - 2}")
+            elif r < TURNED_RUNS:
+                y_bf[r] = sb([P, NODE_RUNS[r], PACK], BF16, f"ybf{r}")
+            else:
+                y_bf[r] = sb([P, NODE_RUNS[r], PACK], BF16, "by_node1")
             copy(
                 y_bf[r][:].rearrange("p (c i) t -> p c t i", i=2),
                 y[r][:].rearrange("p t (c i) -> p c t i", i=2),
             )
 
         def quantise_y(r):
-            nodes = slice(starts[r], starts[r] + NODE_RUNS[r])
             nc.vector.quantize_mx(
-                y_codes[:, nodes].bitcast(E4M3X4), y_scales[:, nodes], y_bf[r][:].rearrange("p x t -> p (x t)")
+                y_codes[:, nodes(r)].bitcast(E4M3X4), y_scales[:, nodes(r)], y_bf[r][:].rearrange("p x t -> p (x t)")
             )
-            nc.sync.dma_start(code_rows[:, nodes], y_codes[:, nodes].bitcast(I32))
+            if r % 2 == 1 or r == final:
+                stored = slice(starts[r - r % 2], nodes(r).stop)
+                nc.sync.dma_start(code_rows[:, stored], y_codes[:, stored].bitcast(I32))
 
-        runs = len(NODE_RUNS)
-        for r in range(runs):
-            gather_dm(r, 0)
-            if r > 0:
-                add_pairs(r - 1)
-                round_y(r - 1, nc.scalar.copy)
-            for t in range(1, PACK):
-                gather_dm(r, t)
-            if r > 1:
-                quantise_y(r - 2)
-        add_pairs(runs - 1)
-        quantise_y(runs - 2)
-        round_y(runs - 1, nc.vector.tensor_copy)
-        quantise_y(runs - 1)
+        final = len(NODE_RUNS) - 1
+        for r in range(final + 1):
+            for t in range(PACK):
+                if t == 0 and r >= TURNED_RUNS:
+                    quantise_y(r - TURNED_RUNS)
+                slot = f"pairs{t}"
+                gather_dm(r, t, slot)
+                if r < TURNED_RUNS:
+                    add_turned(r, t)
+                    if t % 2 == 1:
+                        turn_back(r, t // 2)
+                elif t > 0:
+                    add_pairs(r, t - 1)
+                elif r == final:
+                    add_pairs(r - 1, PACK - 1)
+                    nc.sync.dma_start(y_rows[:, :, nodes(r - 1)], y[r - 1][:])
+                    round_y(r - 1, nc.scalar.copy)
+            if r < TURNED_RUNS:
+                nc.scalar.dma_start(y_rows[:, :, nodes(r)], y[r][:])
+                round_y(r, nc.scalar.copy)
+        add_pairs(final, PACK - 1)
+        nc.sync.dma_start(y_rows[:, :, nodes(final)], y[final][:])
+        quantise_y(final - 2)
+        round_y(final, nc.vector.tensor_copy)
+        quantise_y(final - 1)
+        quantise_y(final)
         for q in range(4):
             queue = nc.scalar if q % 2 == 0 else nc.sync
             queue.dma_start(

@@ -24,8 +24,7 @@ CHUNK = 512
 HALF = CHUNK // 2
 PER_COL = 16
 A0, B0, B1, A1 = 0, 1, 2, 3
-NODE_RUNS = (256, 256, 256, 128, 128)
-TURNED_RUNS = 3
+NODE_RUNS = (256, 256, 256, 256)
 
 
 def tile_attend_gmp_pl_sig_ew_kernel(
@@ -48,7 +47,8 @@ def tile_attend_gmp_pl_sig_ew_kernel(
 
         dy = [sb([P, V], F32, f"dy{t}") for t in range(PACK)]
         ew_rows = {c: sb([P, CHUNK], F32, f"ew{c}") for c in (A0, A1)}
-        square = {c: sb([P, PACK, CHUNK], F32, f"square{c}") for c in (A0, A1)}
+        square = {c: sb([P, 2, CHUNK, 2], F32, f"square{c}") for c in (A0, A1)}
+        h_first = sb([P, PACK, CHUNK], F32, "h_first")
         slope = {(c, t): sb([P, CHUNK], F32, f"slope{c}_{t}") for c in (B0, B1) for t in range(PACK)}
         dz_scales = {c: sb([P, CHUNK], U8, f"dzs{c}") for c in (A0, A1, B0, B1)}
         dm = [sb([P, E], F32, f"dm{t}") for t in range(PACK)]
@@ -93,7 +93,7 @@ def tile_attend_gmp_pl_sig_ew_kernel(
         load_dy(1)
         load_h_plane(B0, 2)
         load_h_plane(B0, 3)
-        nc.sync.dma_start(square[A0][:], h_rows[:, :, edges(A0)])
+        nc.sync.dma_start(h_first[:], h_rows[:, :, edges(A0)])
         load_dy(2)
         nc.sync.dma_start(ew_blocks[:], ew[0:8, :].rearrange("q (c p) -> (q c) p", p=P))
         load_h_plane(B1, 0)
@@ -101,7 +101,11 @@ def tile_attend_gmp_pl_sig_ew_kernel(
         load_h_plane(B1, 2)
         load_h_plane(B1, 3)
         load_dy(3)
-        nc.sync.dma_start(square[A1][:], h_rows[:, :, edges(A1)])
+        h_last = [sb([P, 2, HALF], F32, f"h_last{piece}") for piece in range(4)]
+        for piece in range(4):
+            half, u = divmod(piece, 2)
+            first = A1 * CHUNK + half * HALF
+            nc.sync.dma_start(h_last[piece][:], h_rows[:, 2 * u : 2 * u + 2, first : first + HALF])
         nc.sync.dma_start(src[:], offs2)
 
         nc.vector.tensor_copy(
@@ -113,9 +117,13 @@ def tile_attend_gmp_pl_sig_ew_kernel(
             ws_raw[:].rearrange("p (m t) -> p t m", t=PACK),
         )
 
-        def form_square(c):
-            for t in range(PACK):
-                nc.scalar.activation(square[c][:, t, :], square[c][:, t, :], ACT.Square, bias=minus_half[:])
+        def form_square(c, half, u, h_pair):
+            nc.scalar.activation(
+                square[c][:, u, half * HALF : (half + 1) * HALF, :],
+                h_pair.rearrange("p i e -> p e i"),
+                ACT.Square,
+                bias=minus_half[:],
+            )
 
         def form_slope(c):
             for t in range(PACK):
@@ -125,7 +133,9 @@ def tile_attend_gmp_pl_sig_ew_kernel(
         for c in (A0, A1):
             nc.scalar.activation(ew_rows[c][:], ew_rows[c][:], ACT.Copy, scale=-1.0)
         form_slope(B0)
-        form_square(A0)
+        for half in range(2):
+            for u in range(2):
+                form_square(A0, half, u, h_first[:, 2 * u : 2 * u + 2, half * HALF : (half + 1) * HALF])
         ew_turned = bank([P, P], 7)
         nc.tensor.transpose(ew_turned[:], ew_blocks[:], identity[:])
         nc.scalar.copy(ew_cols[:], ew_turned[:, 0 : E // P])
@@ -136,7 +146,7 @@ def tile_attend_gmp_pl_sig_ew_kernel(
 
         picked = {c: sb([P, PACK, CHUNK], F32, f"picked{c}") for c in (A0, A1)}
         dz_codes = {}
-        dz_whole = {}
+        word_planes = {}
         dz_half = {}
         by_edge = {}
         rounded = {}
@@ -152,21 +162,27 @@ def tile_attend_gmp_pl_sig_ew_kernel(
                     by_edge[c, b] = bank([P, PACK, P], b)
                 nc.tensor.transpose(by_edge[c, b][:, t, :], unweighted[:, b * P : (b + 1) * P], identity[:])
 
-        def form_dz_direct(c, slot):
-            word_planes = sb([P, 2, CHUNK, 2], BF16, slot)
-            for u in range(2):
-                nc.vector.scalar_tensor_tensor(
-                    word_planes[:, u, :, :],
-                    square[c][:, 2 * u : 2 * u + 2, :].rearrange("p i e -> p e i"),
-                    -0.25,
-                    picked[c][:, 2 * u : 2 * u + 2, :].rearrange("p i e -> p e i"),
-                    ALU.add,
-                    ALU.mult,
-                )
-            dz_whole[c] = sb([P, CHUNK, PACK], BF16, f"dz{c}")
-            nc.vector.tensor_copy(
-                dz_whole[c][:].rearrange("p e t -> p (e t)").bitcast(I32).rearrange("p (e u) -> p e u", u=2),
-                word_planes[:].rearrange("p u e i -> p (u e i)").bitcast(I32).rearrange("p (u e) -> p e u", u=2),
+        def product_direct(c, half, u, slot):
+            if (c, half) not in word_planes:
+                word_planes[c, half] = sb([P, 2, HALF, 2], BF16, slot)
+            cols = slice(half * HALF, (half + 1) * HALF)
+            nc.vector.scalar_tensor_tensor(
+                word_planes[c, half][:, u, :, :],
+                square[c][:, u, cols, :],
+                -0.25,
+                picked[c][:, 2 * u : 2 * u + 2, cols].rearrange("p i e -> p e i"),
+                ALU.add,
+                ALU.mult,
+            )
+
+        def weave_direct(c, half, copy):
+            dz_half[c, half] = sb([P, HALF, PACK], BF16, f"dz{c}_{half}")
+            copy(
+                dz_half[c, half][:].rearrange("p e t -> p (e t)").bitcast(I32).rearrange("p (e u) -> p e u", u=2),
+                word_planes[c, half][:]
+                .rearrange("p u e i -> p (u e i)")
+                .bitcast(I32)
+                .rearrange("p (u e) -> p e u", u=2),
             )
 
         def form_dz_turned(c):
@@ -194,15 +210,9 @@ def tile_attend_gmp_pl_sig_ew_kernel(
                     words[:].rearrange("p b u e -> p b e u"),
                 )
 
-        def quantise_whole(c, slot):
-            dz_codes[c] = sb([P, CHUNK], U32, slot)
-            nc.vector.quantize_mx(
-                dz_codes[c][:].bitcast(E5M2X4), dz_scales[c][:], dz_whole[c][:].rearrange("p e t -> p (e t)")
-            )
-
-        def quantise_half(c, half):
+        def quantise_half(c, half, slot=None):
             if half == 0:
-                dz_codes[c] = sb([P, CHUNK], U32, f"dzc{c}")
+                dz_codes[c] = sb([P, CHUNK], U32, slot or f"dzc{c}")
             cols = slice(half * HALF, (half + 1) * HALF)
             nc.vector.quantize_mx(
                 dz_codes[c][:, cols].bitcast(E5M2X4),
@@ -231,27 +241,40 @@ def tile_attend_gmp_pl_sig_ew_kernel(
             if t < PACK - 1:
                 gather_times_slope(B0, t, f"unweighted{t}")
         form_dz_turned(B0)
-        form_square(A1)
-        form_dz_direct(A0, f"slope{B0}_3")
+        for piece in range(4):
+            form_square(A1, piece // 2, piece % 2, h_last[piece][:])
         quantise_half(B0, 0)
-        quantise_whole(A0, f"rounded{B0}_3")
         quantise_half(B0, 1)
         for t in range(PACK):
-            multiply(A0, t, 4 + t, nc.scalar.copy)
-        for t in range(PACK):
             multiply(B0, t, t, nc.scalar.copy)
-        gather_times_slope(B1, 1, f"dz{B0}_0")
-        gather_times_slope(B1, 0, f"dz{A0}")
-        gather_times_slope(B1, 2, f"dz{B0}_1")
-        gather_times_slope(B1, 3, f"slope{B1}_0")
+        gather_times_slope(B1, 0, f"slope{B0}_3")
+        gather_times_slope(B1, 1, f"ew{A0}")
+        gather_times_slope(B1, 2, "h_last1")
+        gather_times_slope(B1, 3, "h_last2")
         form_dz_turned(B1)
-        form_dz_direct(A1, f"slope{B1}_2")
-        quantise_half(B1, 0)
-        quantise_whole(A1, f"rounded{B1}_2")
-        quantise_half(B1, 1)
+        product_direct(A0, 0, 0, f"slope{B1}_2")
+        product_direct(A0, 0, 1, None)
+        product_direct(A0, 1, 0, "h_last3")
+        weave_direct(A0, 0, nc.vector.tensor_copy)
+        product_direct(A0, 1, 1, None)
+        quantise_half(A0, 0, f"rounded{B1}_1")
+        weave_direct(A0, 1, nc.vector.tensor_copy)
+        product_direct(A1, 0, 0, f"slope{B1}_3")
+        quantise_half(A0, 1)
         for t in range(PACK):
-            multiply(A1, t, 6 + t % 2, nc.scalar.copy)
-            multiply(B1, t, 2 + t, nc.vector.tensor_copy if t == 0 else nc.scalar.copy)
+            multiply(A0, t, (6, 7, 0, 1)[t], nc.scalar.copy)
+        quantise_half(B1, 0)
+        quantise_half(B1, 1)
+        product_direct(A1, 0, 1, None)
+        product_direct(A1, 1, 0, f"dz{A0}_1")
+        weave_direct(A1, 0, nc.vector.tensor_copy)
+        product_direct(A1, 1, 1, None)
+        quantise_half(A1, 0)
+        weave_direct(A1, 1, nc.vector.tensor_copy)
+        quantise_half(A1, 1)
+        for t in range(PACK):
+            multiply(B1, t, 2 + t, nc.scalar.copy)
+            multiply(A1, t, (6, 7, 0, 1)[t], nc.vector.tensor_copy if t == 0 else nc.scalar.copy)
 
         y_codes = sb([P, V], U32, "y_codes")
         y_scales = sb([P, V], U8, "y_scales")
@@ -274,7 +297,7 @@ def tile_attend_gmp_pl_sig_ew_kernel(
 
         def add_turned(r, t):
             if t % 2 == 0:
-                sums[r, t // 2] = bank([P, 2, 2, P], (7, 5)[t // 2])
+                sums[r, t // 2] = bank([P, 2, 2, P], (5, 1)[t // 2])
             for b in range(2):
                 for j in range(K):
                     nc.tensor.matmul(
@@ -289,7 +312,7 @@ def tile_attend_gmp_pl_sig_ew_kernel(
         def turn_back(r, u):
             by_node = sb([P, 2 * 2, P], F32, f"by_node{u}")
             nc.scalar.copy(by_node[:], sums[r, u][:].rearrange("x i b p -> x (i b) p"))
-            back = bank([P, 2 * 2, P], u)
+            back = bank([P, 2 * 2, P], 2 + u)
             for piece in range(2 * 2):
                 nc.tensor.transpose(back[:, piece, :], by_node[:, piece, :], identity[:])
             nc.scalar.copy(y[r][:, 2 * u : 2 * u + 2, :], back[:].rearrange("p (i b) x -> p i (b x)", i=2))
@@ -298,13 +321,8 @@ def tile_attend_gmp_pl_sig_ew_kernel(
             both = pairs[r, t][:].rearrange("p (x j) -> p x j", j=K)
             nc.vector.tensor_tensor(y[r][:, t, :], both[:, :, 0], both[:, :, 1], ALU.add)
 
-        def round_y(r, copy):
-            if r == final:
-                y_bf[r] = sb([P, NODE_RUNS[r], PACK], BF16, f"ybf{r - 2}")
-            elif r < TURNED_RUNS:
-                y_bf[r] = sb([P, NODE_RUNS[r], PACK], BF16, f"ybf{r}")
-            else:
-                y_bf[r] = sb([P, NODE_RUNS[r], PACK], BF16, "by_node1")
+        def round_y(r, copy, slot):
+            y_bf[r] = sb([P, NODE_RUNS[r], PACK], BF16, slot)
             copy(
                 y_bf[r][:].rearrange("p (c i) t -> p c t i", i=2),
                 y[r][:].rearrange("p t (c i) -> p c t i", i=2),
@@ -314,34 +332,33 @@ def tile_attend_gmp_pl_sig_ew_kernel(
             nc.vector.quantize_mx(
                 y_codes[:, nodes(r)].bitcast(E4M3X4), y_scales[:, nodes(r)], y_bf[r][:].rearrange("p x t -> p (x t)")
             )
-            if r % 2 == 1 or r == final:
-                stored = slice(starts[r - r % 2], nodes(r).stop)
-                nc.sync.dma_start(code_rows[:, stored], y_codes[:, stored].bitcast(I32))
+            nc.sync.dma_start(code_rows[:, nodes(r)], y_codes[:, nodes(r)].bitcast(I32))
 
         final = len(NODE_RUNS) - 1
-        for r in range(final + 1):
+        for r in range(final):
             for t in range(PACK):
-                if t == 0 and r >= TURNED_RUNS:
-                    quantise_y(r - TURNED_RUNS)
-                slot = f"pairs{t}"
-                gather_dm(r, t, slot)
-                if r < TURNED_RUNS:
-                    add_turned(r, t)
-                    if t % 2 == 1:
-                        turn_back(r, t // 2)
-                elif t > 0:
-                    add_pairs(r, t - 1)
-                elif r == final:
-                    add_pairs(r - 1, PACK - 1)
-                    nc.sync.dma_start(y_rows[:, :, nodes(r - 1)], y[r - 1][:])
-                    round_y(r - 1, nc.scalar.copy)
-            if r < TURNED_RUNS:
-                nc.scalar.dma_start(y_rows[:, :, nodes(r)], y[r][:])
-                round_y(r, nc.scalar.copy)
-        add_pairs(final, PACK - 1)
+                gather_dm(r, t, f"pairs{t}")
+                add_turned(r, t)
+                if t % 2 == 1:
+                    turn_back(r, t // 2)
+                    if r == final - 1:
+                        nc.scalar.dma_start(y_rows[:, t - 1 : t + 1, nodes(r)], y[r][:, t - 1 : t + 1, :])
+            if r < final - 1:
+                nc.sync.dma_start(y_rows[:, :, nodes(r)], y[r][:])
+                round_y(r, nc.scalar.copy, f"ybf{r}")
+        for t in range(2):
+            gather_dm(final, t, f"pairs{t}")
+            add_turned(final, t)
+        turn_back(final, 0)
+        round_y(final - 1, nc.scalar.copy, "by_node0")
+        quantise_y(0)
+        gather_dm(final, 2, "pairs2")
+        gather_dm(final, 3, "pairs3")
+        add_pairs(final, 2)
+        quantise_y(1)
+        add_pairs(final, 3)
         nc.sync.dma_start(y_rows[:, :, nodes(final)], y[final][:])
-        quantise_y(final - 2)
-        round_y(final, nc.vector.tensor_copy)
+        round_y(final, nc.vector.tensor_copy, f"ybf{final}")
         quantise_y(final - 1)
         quantise_y(final)
         for q in range(4):

@@ -82,11 +82,6 @@ def tile_attend_gmp_pl_sig_ew_kernel(
         nc.sync.dma_start(dst[:], offs)
         nc.sync.dma_start(ew_rows[A0][:], ew[:, edges(A0)])
         load_dy(0)
-        nc.scalar.dma_start(w_raw[:].bitcast(I32), w_words[0].bitcast(I32))
-        for q in range(4):
-            nc.scalar.dma_start(
-                ws_raw[32 * q : 32 * q + 4, :].bitcast(I32), w_scales[0, 4 * q : 4 * q + 4, :].bitcast(I32)
-            )
         nc.sync.dma_start(ew_rows[A1][:], ew[:, edges(A1)])
         load_h_plane(B0, 0)
         load_h_plane(B0, 1)
@@ -101,6 +96,11 @@ def tile_attend_gmp_pl_sig_ew_kernel(
         load_h_plane(B1, 2)
         load_h_plane(B1, 3)
         load_dy(3)
+        nc.sync.dma_start(w_raw[:].bitcast(I32), w_words[0].bitcast(I32))
+        for q in range(4):
+            nc.sync.dma_start(
+                ws_raw[32 * q : 32 * q + 4, :].bitcast(I32), w_scales[0, 4 * q : 4 * q + 4, :].bitcast(I32)
+            )
         h_last = [sb([P, 2, HALF], F32, f"h_last{piece}") for piece in range(4)]
         for piece in range(4):
             half, u = divmod(piece, 2)
@@ -332,7 +332,9 @@ def tile_attend_gmp_pl_sig_ew_kernel(
             nc.vector.quantize_mx(
                 y_codes[:, nodes(r)].bitcast(E4M3X4), y_scales[:, nodes(r)], y_bf[r][:].rearrange("p x t -> p (x t)")
             )
-            nc.sync.dma_start(code_rows[:, nodes(r)], y_codes[:, nodes(r)].bitcast(I32))
+            if r != final - 1:
+                stored = slice(starts[r - 1] if r == final else starts[r], nodes(r).stop)
+                nc.sync.dma_start(code_rows[:, stored], y_codes[:, stored].bitcast(I32))
 
         final = len(NODE_RUNS) - 1
         for r in range(final):
@@ -341,10 +343,8 @@ def tile_attend_gmp_pl_sig_ew_kernel(
                 add_turned(r, t)
                 if t % 2 == 1:
                     turn_back(r, t // 2)
-                    if r == final - 1:
-                        nc.scalar.dma_start(y_rows[:, t - 1 : t + 1, nodes(r)], y[r][:, t - 1 : t + 1, :])
+                    (nc.scalar if r == final - 1 else nc.sync).dma_start(y_rows[:, t - 1 : t + 1, nodes(r)], y[r][:, t - 1 : t + 1, :])
             if r < final - 1:
-                nc.sync.dma_start(y_rows[:, :, nodes(r)], y[r][:])
                 round_y(r, nc.scalar.copy, f"ybf{r}")
         for t in range(2):
             gather_dm(final, t, f"pairs{t}")

from contextlib import ExitStack

import concourse.mybir as mybir
from concourse.masks import make_identity

V, K, E, D, DV = 1024, 2, 2048, 512, 512
FLOPS = 2 * DV * D * E

F32 = mybir.dt.float32
BF16 = mybir.dt.bfloat16
I32 = mybir.dt.int32
U32 = mybir.dt.uint32
U16 = mybir.dt.uint16
U8 = mybir.dt.uint8
E2M1X4 = mybir.dt.float4_e2m1fn_x4
E5M2X4 = mybir.dt.float8_e5m2_x4
E4M3X4 = mybir.dt.float8_e4m3fn_x4
ALU = mybir.AluOpType
ACT = mybir.ActivationFunctionType

P = 128
PACK = 4
CHUNK = 512
HALF = CHUNK // 2
PER_COL = 16
A0, B0, B1, A1 = 0, 1, 2, 3
NODE_RUNS = (256, 256, 256, 256)


def tile_attend_gmp_pl_sig_ew_kernel(
    tc, dyT, hE, ew, w_words, w_scales, offs, offs2, out_0, out_1, out_2
):
    nc = tc.nc
    with ExitStack() as ctx:
        lists = ctx.enter_context(tc.tile_pool(name="lists", bufs=1))
        keep = ctx.enter_context(tc.tile_pool(name="keep", bufs=1))
        psum = ctx.enter_context(tc.psum_pool(name="psum", bufs=1))

        def sb(shape, dtype, name):
            return keep.tile(shape, dtype, name=name, align_bytes=64)

        def bank(shape, number):
            return psum.tile(shape, F32, name=f"bank{number}")

        dst = lists.tile([P, E // PER_COL], U16, name="dst")
        src = lists.tile([P, E // PER_COL], U16, name="src")

        dy = [sb([P, V], F32, f"dy{t}") for t in range(PACK)]
        ew_rows = {c: sb([P, CHUNK], F32, f"ew{c}") for c in (A0, A1)}
        square = {c: sb([P, 2, CHUNK, 2], F32, f"square{c}") for c in (A0, A1)}
        h_first = sb([P, PACK, CHUNK], F32, "h_first")
        slope = {(c, t): sb([P, CHUNK], F32, f"slope{c}_{t}") for c in (B0, B1) for t in range(PACK)}
        dz_scales = {c: sb([P, CHUNK], U8, f"dzs{c}") for c in (A0, A1, B0, B1)}
        dm = [sb([P, E], F32, f"dm{t}") for t in range(PACK)]
        w_raw = sb([P, 2 * D], U8, "w_raw")
        ws_raw = sb([P, D], U8, "ws_raw")
        w_dealt = sb([P, 2 * D], U8, "w_dealt")
        ws_dealt = sb([P, D], U8, "ws_dealt")
        ew_blocks = sb([P, P], F32, "ew_blocks")
        ew_cols = sb([P, E // P], F32, "ew_cols")
        minus_half = sb([P, 1], F32, "minus_half")
        quarter = sb([P, 1], F32, "quarter")
        identity = sb([P, P], F32, "identity")

        dy_rows = dyT.rearrange("(p t) v -> p t v", t=PACK)
        h_rows = hE.rearrange("(p t) e -> p t e", t=PACK)

        def edges(c):
            return slice(c * CHUNK, (c + 1) * CHUNK)

        nc.gpsimd.memset(ws_raw[:].bitcast(I32), 0)
        nc.gpsimd.memset(minus_half[:], -0.5)
        make_identity(nc, identity[:])
        nc.scalar.activation(quarter[:], minus_half[:], ACT.Square)

        def load_dy(t):
            nc.sync.dma_start(dy[t][:], dy_rows[:, t, :])

        def load_h_plane(c, t):
            nc.sync.dma_start(slope[c, t][:], h_rows[:, t, edges(c)])

        nc.sync.dma_start(dst[:], offs)
        nc.sync.dma_start(ew_rows[A0][:], ew[:, edges(A0)])
        load_dy(0)
        nc.sync.dma_start(ew_rows[A1][:], ew[:, edges(A1)])
        load_h_plane(B0, 0)
        load_h_plane(B0, 1)
        load_dy(1)
        load_h_plane(B0, 2)
        load_h_plane(B0, 3)
        nc.sync.dma_start(h_first[:], h_rows[:, :, edges(A0)])
        load_dy(2)
        nc.sync.dma_start(ew_blocks[:], ew[0:8, :].rearrange("q (c p) -> (q c) p", p=P))
        load_h_plane(B1, 0)
        load_h_plane(B1, 1)
        load_h_plane(B1, 2)
        load_h_plane(B1, 3)
        load_dy(3)
        nc.sync.dma_start(w_raw[:].bitcast(I32), w_words[0].bitcast(I32))
        for q in range(4):
            nc.sync.dma_start(
                ws_raw[32 * q : 32 * q + 4, :].bitcast(I32), w_scales[0, 4 * q : 4 * q + 4, :].bitcast(I32)
            )
        h_last = [sb([P, 2, HALF], F32, f"h_last{piece}") for piece in range(4)]
        for piece in range(4):
            half, u = divmod(piece, 2)
            first = A1 * CHUNK + half * HALF
            nc.sync.dma_start(h_last[piece][:], h_rows[:, 2 * u : 2 * u + 2, first : first + HALF])
        nc.sync.dma_start(src[:], offs2)

        nc.vector.tensor_copy(
            w_dealt[:].bitcast(U16).rearrange("p (t m) -> p t m", t=PACK),
            w_raw[:].bitcast(U16).rearrange("p (m t) -> p t m", t=PACK),
        )
        nc.vector.tensor_copy(
            ws_dealt[:].rearrange("p (t m) -> p t m", t=PACK),
            ws_raw[:].rearrange("p (m t) -> p t m", t=PACK),
        )

        def form_square(c, half, u, h_pair):
            nc.scalar.activation(
                square[c][:, u, half * HALF : (half + 1) * HALF, :],
                h_pair.rearrange("p i e -> p e i"),
                ACT.Square,
                bias=minus_half[:],
            )

        def form_slope(c):
            for t in range(PACK):
                nc.scalar.activation(slope[c, t][:], slope[c, t][:], ACT.Square, bias=minus_half[:])
                nc.scalar.activation(slope[c, t][:], slope[c, t][:], ACT.Identity, bias=quarter[:], scale=-1.0)

        for c in (A0, A1):
            nc.scalar.activation(ew_rows[c][:], ew_rows[c][:], ACT.Copy, scale=-1.0)
        form_slope(B0)
        for half in range(2):
            for u in range(2):
                form_square(A0, half, u, h_first[:, 2 * u : 2 * u + 2, half * HALF : (half + 1) * HALF])
        ew_turned = bank([P, P], 7)
        nc.tensor.transpose(ew_turned[:], ew_blocks[:], identity[:])
        nc.scalar.copy(ew_cols[:], ew_turned[:, 0 : E // P])
        form_slope(B1)

        def listed(c):
            return dst[:, c * CHUNK // PER_COL : (c + 1) * CHUNK // PER_COL]

        picked = {c: sb([P, PACK, CHUNK], F32, f"picked{c}") for c in (A0, A1)}
        dz_codes = {}
        word_planes = {}
        dz_half = {}
        by_edge = {}
        rounded = {}

        def gather_times_weight(c, t):
            nc.vector.tensor_tensor(picked[c][:, t, :], dy[t][:].indirect(listed(c)), ew_rows[c][:], ALU.mult)

        def gather_times_slope(c, t, slot):
            unweighted = sb([P, CHUNK], F32, slot)
            nc.vector.tensor_tensor(unweighted[:], dy[t][:].indirect(listed(c)), slope[c, t][:], ALU.mult)
            for b in range(CHUNK // P):
                if (c, b) not in by_edge:
                    by_edge[c, b] = bank([P, PACK, P], b)
                nc.tensor.transpose(by_edge[c, b][:, t, :], unweighted[:, b * P : (b + 1) * P], identity[:])

        def product_direct(c, half, u, slot):
            if (c, half) not in word_planes:
                word_planes[c, half] = sb([P, 2, HALF, 2], BF16, slot)
            cols = slice(half * HALF, (half + 1) * HALF)
            nc.vector.scalar_tensor_tensor(
                word_planes[c, half][:, u, :, :],
                square[c][:, u, cols, :],
                -0.25,
                picked[c][:, 2 * u : 2 * u + 2, cols].rearrange("p i e -> p e i"),
                ALU.add,
                ALU.mult,
            )

        def weave_direct(c, half, copy):
            dz_half[c, half] = sb([P, HALF, PACK], BF16, f"dz{c}_{half}")
            copy(
                dz_half[c, half][:].rearrange("p e t -> p (e t)").bitcast(I32).rearrange("p (e u) -> p e u", u=2),
                word_planes[c, half][:]
                .rearrange("p u e i -> p (u e i)")
                .bitcast(I32)
                .rearrange("p (u e) -> p e u", u=2),
            )

        def form_dz_turned(c):
            for half in range(2):
                words = bank([P, 2, 2, P], 4 + half)
                for bb in range(2):
                    b = 2 * half + bb
                    rounded[c, b] = sb([P, 2, P, 2], BF16, f"rounded{c}_{b}")
                    column = c * (CHUNK // P) + b
                    nc.scalar.activation(
                        rounded[c, b][:],
                        by_edge[c, b][:].rearrange("e (u i) p -> e u p i", i=2),
                        ACT.Copy,
                        scale=ew_cols[:, column : column + 1],
                    )
                    as_words = rounded[c, b][:].rearrange("e u p i -> e (u p i)").bitcast(F32)
                    for u in range(2):
                        nc.tensor.transpose(words[:, bb, u, :], as_words[:, u * P : (u + 1) * P], identity[:])
                dz_half[c, half] = sb([P, HALF, PACK], BF16, f"dz{c}_{half}")
                nc.scalar.copy(
                    dz_half[c, half][:]
                    .rearrange("p e t -> p (e t)")
                    .bitcast(F32)
                    .rearrange("p (b e u) -> p b e u", b=2, u=2),
                    words[:].rearrange("p b u e -> p b e u"),
                )

        def quantise_half(c, half, slot=None):
            if half == 0:
                dz_codes[c] = sb([P, CHUNK], U32, slot or f"dzc{c}")
            cols = slice(half * HALF, (half + 1) * HALF)
            nc.vector.quantize_mx(
                dz_codes[c][:, cols].bitcast(E5M2X4),
                dz_scales[c][:, cols],
                dz_half[c, half][:].rearrange("p e t -> p (e t)"),
            )

        def multiply(c, t, number, copy):
            acc = bank([P, CHUNK], number)
            nc.tensor.matmul_mx(
                acc[:],
                lhsT=w_dealt[:, t * 2 * P : (t + 1) * 2 * P].bitcast(E2M1X4),
                lhsT_scale=ws_dealt[:, t * P : (t + 1) * P],
                rhs=dz_codes[c][:].bitcast(E5M2X4),
                rhs_scale=dz_scales[c][:],
                start=True,
                stop=True,
            )
            copy(dm[t][:, edges(c)], acc[:])

        for t in range(PACK):
            if t == PACK - 1:
                gather_times_slope(B0, t, f"unweighted{t}")
            gather_times_weight(A0, t)
            gather_times_weight(A1, t)
            if t < PACK - 1:
                gather_times_slope(B0, t, f"unweighted{t}")
        form_dz_turned(B0)
        for piece in range(4):
            form_square(A1, piece // 2, piece % 2, h_last[piece][:])
        quantise_half(B0, 0)
        quantise_half(B0, 1)
        for t in range(PACK):
            multiply(B0, t, t, nc.scalar.copy)
        gather_times_slope(B1, 0, f"slope{B0}_3")
        gather_times_slope(B1, 1, f"ew{A0}")
        gather_times_slope(B1, 2, "h_last1")
        gather_times_slope(B1, 3, "h_last2")
        form_dz_turned(B1)
        product_direct(A0, 0, 0, f"slope{B1}_2")
        product_direct(A0, 0, 1, None)
        product_direct(A0, 1, 0, "h_last3")
        weave_direct(A0, 0, nc.vector.tensor_copy)
        product_direct(A0, 1, 1, None)
        quantise_half(A0, 0, f"rounded{B1}_1")
        weave_direct(A0, 1, nc.vector.tensor_copy)
        product_direct(A1, 0, 0, f"slope{B1}_3")
        quantise_half(A0, 1)
        for t in range(PACK):
            multiply(A0, t, (6, 7, 0, 1)[t], nc.scalar.copy)
        quantise_half(B1, 0)
        quantise_half(B1, 1)
        product_direct(A1, 0, 1, None)
        product_direct(A1, 1, 0, f"dz{A0}_1")
        weave_direct(A1, 0, nc.vector.tensor_copy)
        product_direct(A1, 1, 1, None)
        quantise_half(A1, 0)
        weave_direct(A1, 1, nc.vector.tensor_copy)
        quantise_half(A1, 1)
        for t in range(PACK):
            multiply(B1, t, 2 + t, nc.scalar.copy)
            multiply(A1, t, (6, 7, 0, 1)[t], nc.vector.tensor_copy if t == 0 else nc.scalar.copy)

        y_codes = sb([P, V], U32, "y_codes")
        y_scales = sb([P, V], U8, "y_scales")
        y_rows = out_0.rearrange("(p t) x -> p t x", t=PACK)
        code_rows = out_1[0].rearrange("p x l -> p (x l)").bitcast(I32)

        starts = [sum(NODE_RUNS[:r]) for r in range(len(NODE_RUNS))]
        y = [sb([P, PACK, n], F32, f"y{r}") for r, n in enumerate(NODE_RUNS)]
        pairs = {}
        y_bf = {}
        sums = {}

        def nodes(r):
            return slice(starts[r], starts[r] + NODE_RUNS[r])

        def gather_dm(r, t, slot):
            pairs[r, t] = sb([P, K * NODE_RUNS[r]], F32, slot)
            cols = slice(K * starts[r] // PER_COL, K * (starts[r] + NODE_RUNS[r]) // PER_COL)
            nc.vector.tensor_copy(pairs[r, t][:], dm[t][:].indirect(src[:, cols]))

        def add_turned(r, t):
            if t % 2 == 0:
                sums[r, t // 2] = bank([P, 2, 2, P], (5, 1)[t // 2])
            for b in range(2):
                for j in range(K):
                    nc.tensor.matmul(
                        sums[r, t // 2][:, t % 2, b, :],
                        lhsT=pairs[r, t][:, b * K * P + j : (b + 1) * K * P : K],
                        rhs=identity[:],
                        is_transpose=True,
                        start=(j == 0),
                        stop=(j == K - 1),
                    )

        def turn_back(r, u):
            by_node = sb([P, 2 * 2, P], F32, f"by_node{u}")
            nc.scalar.copy(by_node[:], sums[r, u][:].rearrange("x i b p -> x (i b) p"))
            back = bank([P, 2 * 2, P], 2 + u)
            for piece in range(2 * 2):
                nc.tensor.transpose(back[:, piece, :], by_node[:, piece, :], identity[:])
            nc.scalar.copy(y[r][:, 2 * u : 2 * u + 2, :], back[:].rearrange("p (i b) x -> p i (b x)", i=2))

        def add_pairs(r, t):
            both = pairs[r, t][:].rearrange("p (x j) -> p x j", j=K)
            nc.vector.tensor_tensor(y[r][:, t, :], both[:, :, 0], both[:, :, 1], ALU.add)

        def round_y(r, copy, slot):
            y_bf[r] = sb([P, NODE_RUNS[r], PACK], BF16, slot)
            copy(
                y_bf[r][:].rearrange("p (c i) t -> p c t i", i=2),
                y[r][:].rearrange("p t (c i) -> p c t i", i=2),
            )

        def quantise_y(r):
            nc.vector.quantize_mx(
                y_codes[:, nodes(r)].bitcast(E4M3X4), y_scales[:, nodes(r)], y_bf[r][:].rearrange("p x t -> p (x t)")
            )
            if r != final - 1:
                stored = slice(starts[r - 1] if r == final else starts[r], nodes(r).stop)
                nc.sync.dma_start(code_rows[:, stored], y_codes[:, stored].bitcast(I32))

        final = len(NODE_RUNS) - 1
        for r in range(final):
            for t in range(PACK):
                gather_dm(r, t, f"pairs{t}")
                add_turned(r, t)
                if t % 2 == 1:
                    turn_back(r, t // 2)
                    (nc.scalar if r == final - 1 else nc.sync).dma_start(y_rows[:, t - 1 : t + 1, nodes(r)], y[r][:, t - 1 : t + 1, :])
            if r < final - 1:
                round_y(r, nc.scalar.copy, f"ybf{r}")
        for t in range(2):
            gather_dm(final, t, f"pairs{t}")
            add_turned(final, t)
        turn_back(final, 0)
        round_y(final - 1, nc.scalar.copy, "by_node0")
        quantise_y(0)
        gather_dm(final, 2, "pairs2")
        gather_dm(final, 3, "pairs3")
        add_pairs(final, 2)
        quantise_y(1)
        add_pairs(final, 3)
        nc.sync.dma_start(y_rows[:, :, nodes(final)], y[final][:])
        round_y(final, nc.vector.tensor_copy, f"ybf{final}")
        quantise_y(final - 1)
        quantise_y(final)
        for q in range(4):
            queue = nc.scalar if q % 2 == 0 else nc.sync
            queue.dma_start(
                out_2[0, 4 * q : 4 * q + 4, :].bitcast(I32), y_scales[32 * q : 32 * q + 4, :].bitcast(I32)
            )
